import numpy as np
import ml_dtypes


def mxq(x, axis, fmt="e4m3"):
    dtype, down = {"e4m3": (ml_dtypes.float8_e4m3fn, 7), "e5m2": (ml_dtypes.float8_e5m2, 14)}[fmt]
    v = np.moveaxis(np.asarray(x, np.float32).astype(ml_dtypes.bfloat16).astype(np.float64), axis, -1)
    blocks = v.reshape(v.shape[:-1] + (-1, 32))
    amax = np.abs(blocks).max(-1, keepdims=True)
    byte = np.maximum(np.where(amax > 0, np.frexp(amax)[1] - 1 + 127, 0) - down, 1)
    scale = np.exp2(byte - 127.0)
    codes = (blocks / scale).astype(np.float32).astype(dtype).astype(np.float64)
    return np.moveaxis((codes * scale).reshape(v.shape), -1, axis)


WIDE = False


def mx_kscale(k):
    if not WIDE:
        return np.ones(k)
    levels = np.array([10, -10, 5, -5, 0])
    if k % 512:
        return np.exp2(np.random.permutation(np.resize(levels, k // 32))).repeat(32)
    a = np.empty((k // 512, 16))
    for p in range(k // 512):
        a[p, :8] = np.random.permutation(np.resize(levels, 8))
        for g in range(8):
            far = levels[np.abs(levels - a[p, g]) >= 10]
            a[p, g + 8] = far[np.random.randint(len(far))]
    return np.exp2(a.ravel()).repeat(32)


def f64(x):
    return np.asarray(x).astype(np.float64)


def striped(idx):
    return np.tile(idx.reshape(-1, 16).T, (8, 1)).astype(np.uint16)


def unstriped(offs):
    return offs[:16].T.reshape(-1).astype(np.int64)


def striped8(idx):
    return np.concatenate([x.reshape(-1, 16).T for x in idx]).astype(np.uint16)


def runs(offs, k):
    lists = np.stack([offs[16 * r : 16 * r + 16].T.reshape(-1) for r in range(8)]).astype(np.int64)
    return lists[np.arange(k) % 512 // 64]


def pack_weight(w):
    k, n = w.shape
    w = f64(np.asarray(w, np.float32).astype(ml_dtypes.bfloat16)).reshape(k // 32, 32, n)
    amax = np.abs(w).max(1)
    byte = np.clip(np.where(amax > 0, np.frexp(amax)[1] - 1 + 127 - 7, 1), 1, 254)
    scaled = (w * np.exp2(127.0 - byte)[:, None, :]).reshape(k, n).astype(np.float32)
    words = np.ascontiguousarray(scaled.reshape(k // 512, 128, 4, n).transpose(0, 1, 3, 2)).astype(ml_dtypes.float8_e4m3fn).view(np.uint8)
    return words, np.ascontiguousarray(byte.astype(np.uint8).reshape(k // 512, 16, n))


def unpack_weight(words, scales):
    g, p, n, _ = words.shape
    vals = np.ascontiguousarray(words).view(ml_dtypes.float8_e4m3fn).astype(np.float64) * np.repeat(np.exp2(scales.astype(np.float64) - 127.0), 8, axis=1)[..., None]
    return vals.transpose(0, 1, 3, 2).reshape(g * 512, n)


K, T, S, V, N, H = 512, 2048, 512, 128, 512, 512


def setup_inputs():
    n = np.random.standard_normal
    s = mx_kscale(K)[:, None]
    u = mx_kscale(H)
    packed_xT = pack_weight(n((K, T)) * s)
    perm = np.stack([np.random.permutation(S) for _ in range(8)])
    return {
        "x_words": packed_xT[0],
        "x_scales": packed_xT[1],
        "w1": (n((K, H)) / np.sqrt(K) / s * u).astype(np.float32),
        "w2": (n((H, N)) / np.sqrt(H) / u[:, None]).astype(np.float32),
        "offs": striped(np.random.permutation(T)[:S]),
        "la": striped8(perm[:, :V]),
        "lb": striped8(perm[:, V:2 * V]),
        "lc": striped8(perm[:, 2 * V:3 * V]),
        "ld": striped8(perm[:, 3 * V:]),
    }


def reference(x_words, x_scales, w1, w2, offs, la, lb, lc, ld):
    xq = unpack_weight(x_words, x_scales)[:, unstriped(offs)]
    y = mxq(f64(w1), 0, "e4m3").T @ xq
    b = y[np.arange(H)[:, None], runs(lb, H)]
    d = y[np.arange(H)[:, None], runs(ld, H)]
    n3 = np.minimum(b, d)
    c = y[np.arange(H)[:, None], runs(lc, H)]
    n2 = c + d
    a = y[np.arange(H)[:, None], runs(la, H)]
    n1 = np.maximum(a, b)
    n0 = a - c
    p0 = np.zeros((H, S))
    p0[np.arange(H)[:, None], runs(la, H)] = n0
    p = p0.copy()
    p[np.arange(H)[:, None], runs(lb, H)] = n1
    p2 = p.copy()
    p2[np.arange(H)[:, None], runs(lc, H)] = n2
    z = p2.copy()
    z[np.arange(H)[:, None], runs(ld, H)] = n3
    return mxq(f64(w2), 0, "e4m3").T @ mxq(z, 0, "e4m3")

@@ -1,0 +1,160 @@
+from contextlib import ExitStack
+
+import concourse.mybir as mybir
+
+K, T, S, V, N, H = 512, 2048, 512, 128, 512, 512
+FLOPS = 2 * K * H * S + 2 * H * N * S
+
+F32 = mybir.dt.float32
+BF16 = mybir.dt.bfloat16
+I32 = mybir.dt.int32
+U32 = mybir.dt.uint32
+U16 = mybir.dt.uint16
+U8 = mybir.dt.uint8
+FP8X4 = mybir.dt.float8_e4m3fn_x4
+ALU = mybir.AluOpType
+COPY = mybir.ActivationFunctionType.Copy
+
+P = 128
+PACK = 4
+HALF = S // 2
+W1_VECTOR_SHARE = 80
+
+
+def tile_picked_quart4_none_p_kernel(tc, x_words, x_scales, w1, w2, offs, la, lb, lc, ld, out):
+    nc = tc.nc
+    with ExitStack() as ctx:
+        keep = ctx.enter_context(tc.tile_pool(name="keep", bufs=1))
+        psum = ctx.enter_context(tc.psum_pool(name="psum", bufs=8))
+
+        offs_sb = keep.tile([P, S // 16], U16, name="offs_sb")
+        nc.sync.dma_start(offs_sb[:], offs)
+
+        lists = {}
+
+        def load_list(key, src):
+            lists[key] = keep.tile([P, V // 16], U16, name="list_" + key)
+            nc.sync.dma_start(lists[key][:], src)
+
+        for key, src in (("c", lc), ("a", la), ("d", ld)):
+            load_list(key, src)
+
+        scale_table = keep.tile([P, T], U8, name="scale_table")
+        nc.vector.memset(scale_table[:].bitcast(I32), 0)
+        for q in range(4):
+            nc.scalar.dma_start(scale_table[32 * q : 32 * q + 4, :].bitcast(I32), x_scales[0, 4 * q : 4 * q + 4, :].bitcast(I32))
+
+        w1_raw = keep.tile([P, PACK, H], F32, name="w1_raw", tag="w_raw")
+        nc.sync.dma_start(w1_raw[:], w1.rearrange("(p j) c -> p j c", j=PACK))
+        word_table = keep.tile([P, T], U32, name="word_table")
+        nc.sync.dma_start(word_table[:].bitcast(I32), x_words[0].rearrange("p n t -> p (n t)").bitcast(I32))
+
+        load_list("b", lb)
+
+        x_sc = keep.tile([P, S], U8, name="x_sc", align_bytes=64)
+        nc.vector.tensor_copy(x_sc[:], scale_table[:].indirect(offs_sb[:]))
+
+        w1_bf = keep.tile([P, PACK, P, PACK], BF16, name="w1_bf", align_bytes=64)
+        w1_src = w1_raw[:].rearrange("p j (m t) -> p m j t", t=PACK)
+        w1_dst = w1_bf[:].rearrange("p t m j -> p m j t")
+        nc.vector.tensor_copy(w1_dst[:, :W1_VECTOR_SHARE], w1_src[:, :W1_VECTOR_SHARE])
+        nc.scalar.copy(w1_dst[:, W1_VECTOR_SHARE:], w1_src[:, W1_VECTOR_SHARE:])
+        w1_codes = keep.tile([P, PACK, P], U32, name="w1_codes", align_bytes=64)
+        w1_sc = keep.tile([P, PACK, P], U8, name="w1_sc", align_bytes=64)
+        for t in range(PACK):
+            nc.vector.quantize_mx(w1_codes[:, t, :].bitcast(FP8X4), w1_sc[:, t, :], w1_bf[:, t].rearrange("p m j -> p (m j)"))
+
+        w2_raw = keep.tile([P, PACK, N], F32, name="w2_raw", tag="w_raw")
+        nc.sync.dma_start(w2_raw[:], w2.rearrange("(p j) c -> p j c", j=PACK))
+
+        x_codes = keep.tile([P, S], U32, name="x_codes", align_bytes=64)
+        for h in range(2):
+            nc.vector.tensor_copy(x_codes[:, h * HALF : (h + 1) * HALF], word_table[:].indirect(offs_sb[:, h * 16 : (h + 1) * 16]))
+
+        y = [keep.tile([P, S], F32, name="y%d" % t) for t in range(PACK)]
+        for t in range(PACK):
+            width = HALF if t == 0 else S
+            for c0 in range(0, S, width):
+                cols = slice(c0, c0 + width)
+                acc = psum.tile([P, S], F32, name="acc", tag="bank")
+                nc.tensor.matmul_mx(acc[:, :width], w1_codes[:, t, :].bitcast(FP8X4), w1_sc[:, t, :], x_codes[:, cols].bitcast(FP8X4), x_sc[:, cols], start=True, stop=True)
+                nc.scalar.copy(y[t][:, cols], acc[:, :width])
+
+        got = {}
+        z = [keep.tile([P, S], F32, name="z%d" % t) for t in range(PACK)]
+        z_bf = [keep.tile([P, HALF, PACK], BF16, name="z_bf%d" % h, align_bytes=64) for h in range(2)]
+
+        def gather(t):
+            for key in "cadb":
+                got[key, t] = keep.tile([P, V], F32, name="got_%s%d" % (key, t))
+                nc.vector.tensor_copy(got[key, t][:], y[t][:].indirect(lists[key][:]))
+                if key == "c":
+                    got["minus_c", t] = keep.tile([P, V], F32, name="minus_c%d" % t)
+                    nc.scalar.activation(got["minus_c", t][:], got["c", t][:], COPY, scale=-1.0)
+            got["max", t] = keep.tile([P, V], F32, name="larger%d" % t)
+            got["min", t] = keep.tile([P, V], F32, name="smaller%d" % t)
+
+        def combine(t):
+            nc.vector.tensor_tensor(got["max", t][:], got["a", t][:], got["b", t][:], ALU.max)
+            nc.vector.tensor_tensor(got["min", t][:], got["b", t][:], got["d", t][:], ALU.min)
+
+        def scatter(t, key):
+            window = z[t][:].indirect(lists[key][:])
+            if key == "a":
+                nc.vector.tensor_tensor(window, got["a", t][:], got["minus_c", t][:], ALU.add)
+            elif key == "c":
+                nc.vector.tensor_tensor(window, got["c", t][:], got["d", t][:], ALU.add)
+            else:
+                nc.vector.tensor_copy(window, got["max" if key == "b" else "min", t][:])
+
+        def lay(t, h, engine_copy):
+            cols = slice(h * HALF, (h + 1) * HALF)
+            if t == 2:
+                engine_copy(z_bf[h][:, :, 2:4], z[t][:, cols].unsqueeze(2).to_broadcast([P, HALF, 2]))
+            else:
+                engine_copy(z_bf[h][:, :, t], z[t][:, cols])
+
+        w2_bf = keep.tile([P, N, PACK], BF16, name="w2_bf", align_bytes=64)
+        w2_codes = keep.tile([P, N], U32, name="w2_codes", align_bytes=64)
+        w2_sc = keep.tile([P, N], U8, name="w2_sc", align_bytes=64)
+
+        gather(0)
+        gather(1)
+        combine(0)
+        for u in range(PACK):
+            cols = slice(u * P, (u + 1) * P)
+            nc.scalar.copy(w2_bf[:, cols, :].rearrange("p (c i) j -> p c j i", i=4), w2_raw[:, :, cols].rearrange("p j (c i) -> p c j i", i=4))
+        combine(1)
+        gather(2)
+        gather(3)
+        combine(2)
+        combine(3)
+        done = [0] * PACK
+        for step, t in enumerate((0, 1, 0, 1, 0, 1, 0, 2, 1, 2, 3, 2, 3, 2, 3, 3)):
+            if step == 15:
+                nc.vector.quantize_mx(w2_codes[:].bitcast(FP8X4), w2_sc[:], w2_bf[:].rearrange("p m j -> p (m j)"))
+            scatter(t, "cabd"[done[t]])
+            done[t] = done[t] + 1
+            if done[t] == 4 and t < 3:
+                lay(t, 0, nc.scalar.copy)
+                lay(t, 1, nc.scalar.copy)
+        lay(3, 0, nc.vector.tensor_copy)
+        lay(3, 1, nc.scalar.copy)
+
+        z_codes = keep.tile([P, S], U32, name="z_codes", align_bytes=64)
+        z_sc = keep.tile([P, S], U8, name="z_sc", align_bytes=64)
+        out_rows = out.rearrange("(u p) j -> p u j", p=P)
+        for h in range(2):
+            cols = slice(h * HALF, (h + 1) * HALF)
+            nc.vector.quantize_mx(z_codes[:, cols].bitcast(FP8X4), z_sc[:, cols], z_bf[h][:].rearrange("p c j -> p (c j)"))
+        for h in range(2):
+            cols = slice(h * HALF, (h + 1) * HALF)
+            for pair in range(2):
+                acc = psum.tile([P, S], F32, name="acc", tag="bank")
+                for e in range(2):
+                    rows = slice((2 * pair + e) * P, (2 * pair + e + 1) * P)
+                    nc.tensor.matmul_mx(acc[:, e * HALF : (e + 1) * HALF], w2_codes[:, rows].bitcast(FP8X4), w2_sc[:, rows], z_codes[:, cols].bitcast(FP8X4), z_sc[:, cols], start=True, stop=True)
+                res = keep.tile([P, 2, HALF], F32, name="res%d%d" % (h, pair))
+                copy = nc.scalar.copy if pair == 0 else nc.vector.tensor_copy
+                copy(res[:].rearrange("p e c -> p (e c)"), acc[:])
+                nc.sync.dma_start(out_rows[:, 2 * pair : 2 * pair + 2, cols], res[:])

@@ -18,7 +18,6 @@ COPY = mybir.ActivationFunctionType.Copy
 P = 128
 PACK = 4
 HALF = S // 2
-W1_VECTOR_SHARE = 80
 
 
 def tile_picked_quart4_none_p_kernel(tc, x_words, x_scales, w1, w2, offs, la, lb, lc, ld, out):
@@ -27,75 +26,80 @@ def tile_picked_quart4_none_p_kernel(tc, x_words, x_scales, w1, w2, offs, la, lb
         keep = ctx.enter_context(tc.tile_pool(name="keep", bufs=1))
         psum = ctx.enter_context(tc.psum_pool(name="psum", bufs=8))
 
-        offs_sb = keep.tile([P, S // 16], U16, name="offs_sb")
-        nc.sync.dma_start(offs_sb[:], offs)
+        def sbuf(shape, dtype, name, tag=None):
+            return keep.tile(shape, dtype, name=name, tag=tag or name, align_bytes=64)
 
         lists = {}
 
-        def load_list(key, src):
-            lists[key] = keep.tile([P, V // 16], U16, name="list_" + key)
+        def load_list(key, src, entries):
+            lists[key] = sbuf([P, entries // 16], U16, "list_" + key)
             nc.sync.dma_start(lists[key][:], src)
 
-        for key, src in (("c", lc), ("a", la), ("d", ld)):
-            load_list(key, src)
+        load_list("offs", offs, S)
 
-        scale_table = keep.tile([P, T], U8, name="scale_table")
+        word_table = sbuf([P, T], U32, "word_table")
+        nc.sync.dma_start(word_table[:].bitcast(I32), x_words[0].rearrange("p n t -> p (n t)").bitcast(I32))
+        w1_raw = sbuf([P, PACK, H], F32, "w1_raw", "w_raw")
+        nc.sync.dma_start(w1_raw[:], w1.rearrange("(p j) c -> p j c", j=PACK))
+        scale_table = sbuf([P, T], U8, "scale_table")
         nc.vector.memset(scale_table[:].bitcast(I32), 0)
         for q in range(4):
-            nc.scalar.dma_start(scale_table[32 * q : 32 * q + 4, :].bitcast(I32), x_scales[0, 4 * q : 4 * q + 4, :].bitcast(I32))
+            nc.sync.dma_start(scale_table[32 * q : 32 * q + 4, :].bitcast(I32), x_scales[0, 4 * q : 4 * q + 4, :].bitcast(I32))
+        for key, src in (("c", lc), ("a", la), ("d", ld), ("b", lb)):
+            load_list(key, src, V)
 
-        w1_raw = keep.tile([P, PACK, H], F32, name="w1_raw", tag="w_raw")
-        nc.sync.dma_start(w1_raw[:], w1.rearrange("(p j) c -> p j c", j=PACK))
-        word_table = keep.tile([P, T], U32, name="word_table")
-        nc.sync.dma_start(word_table[:].bitcast(I32), x_words[0].rearrange("p n t -> p (n t)").bitcast(I32))
+        x_codes = sbuf([P, S], U32, "x_codes")
+        nc.vector.tensor_copy(x_codes[:], word_table[:].indirect(lists["offs"][:]))
 
-        load_list("b", lb)
-
-        x_sc = keep.tile([P, S], U8, name="x_sc", align_bytes=64)
-        nc.vector.tensor_copy(x_sc[:], scale_table[:].indirect(offs_sb[:]))
-
-        w1_bf = keep.tile([P, PACK, P, PACK], BF16, name="w1_bf", align_bytes=64)
-        w1_src = w1_raw[:].rearrange("p j (m t) -> p m j t", t=PACK)
-        w1_dst = w1_bf[:].rearrange("p t m j -> p m j t")
-        nc.vector.tensor_copy(w1_dst[:, :W1_VECTOR_SHARE], w1_src[:, :W1_VECTOR_SHARE])
-        nc.scalar.copy(w1_dst[:, W1_VECTOR_SHARE:], w1_src[:, W1_VECTOR_SHARE:])
-        w1_codes = keep.tile([P, PACK, P], U32, name="w1_codes", align_bytes=64)
-        w1_sc = keep.tile([P, PACK, P], U8, name="w1_sc", align_bytes=64)
+        w1_src = w1_raw[:].rearrange("p j (g t s i) -> p t g s j i", t=PACK, s=2, i=4)
+        w1_bf, w1_codes, w1_sc = {}, {}, {}
         for t in range(PACK):
-            nc.vector.quantize_mx(w1_codes[:, t, :].bitcast(FP8X4), w1_sc[:, t, :], w1_bf[:, t].rearrange("p m j -> p (m j)"))
+            w1_bf[t] = sbuf([P, P, PACK], BF16, "w1_bf%d" % t)
+            engine_copy = nc.vector.tensor_copy if t == 0 else nc.scalar.copy
+            engine_copy(w1_bf[t][:].rearrange("p (g s i) j -> p g s j i", s=2, i=4), w1_src[:, t])
 
-        w2_raw = keep.tile([P, PACK, N], F32, name="w2_raw", tag="w_raw")
-        nc.sync.dma_start(w2_raw[:], w2.rearrange("(p j) c -> p j c", j=PACK))
+        def quantize_w1(t):
+            w1_codes[t] = sbuf([P, P], U32, "w1_codes%d" % t)
+            w1_sc[t] = sbuf([P, P], U8, "w1_sc%d" % t)
+            nc.vector.quantize_mx(w1_codes[t][:].bitcast(FP8X4), w1_sc[t][:], w1_bf[t][:].rearrange("p m j -> p (m j)"))
 
-        x_codes = keep.tile([P, S], U32, name="x_codes", align_bytes=64)
+        x_sc = sbuf([P, S], U8, "x_sc")
         for h in range(2):
-            nc.vector.tensor_copy(x_codes[:, h * HALF : (h + 1) * HALF], word_table[:].indirect(offs_sb[:, h * 16 : (h + 1) * 16]))
+            nc.vector.tensor_copy(x_sc[:, h * HALF : (h + 1) * HALF], scale_table[:].indirect(lists["offs"][:, h * 16 : (h + 1) * 16]))
+            quantize_w1(h)
+        quantize_w1(2)
+        quantize_w1(3)
 
-        y = [keep.tile([P, S], F32, name="y%d" % t) for t in range(PACK)]
+        raw_tags = ("w_raw", "word_table")
+        w2_raw = [sbuf([P, PACK, N // 2], F32, "w2_raw%d" % h, raw_tags[h]) for h in range(2)]
+        w2_rows = w2.rearrange("(g t s) (h c) -> s h g t c", t=PACK, s=8, h=2)
+        for s in range(8):
+            for h in range(2):
+                nc.sync.dma_start(w2_raw[h][s:P:8, :, :], w2_rows[s, h])
+
+        y = [sbuf([P, S], F32, "y%d" % t) for t in range(PACK)]
         for t in range(PACK):
-            width = HALF if t == 0 else S
-            for c0 in range(0, S, width):
+            for c0, width in ((0, HALF), (HALF, P), (HALF + P, P)) if t == 0 else ((0, S),):
                 cols = slice(c0, c0 + width)
                 acc = psum.tile([P, S], F32, name="acc", tag="bank")
-                nc.tensor.matmul_mx(acc[:, :width], w1_codes[:, t, :].bitcast(FP8X4), w1_sc[:, t, :], x_codes[:, cols].bitcast(FP8X4), x_sc[:, cols], start=True, stop=True)
-                nc.scalar.copy(y[t][:, cols], acc[:, :width])
+                nc.tensor.matmul_mx(acc[:, :width], w1_codes[t][:].bitcast(FP8X4), w1_sc[t][:], x_codes[:, cols].bitcast(FP8X4), x_sc[:, cols], start=True, stop=True)
+                engine_copy = nc.vector.tensor_copy if c0 > HALF else nc.scalar.copy
+                engine_copy(y[t][:, cols], acc[:, :width])
 
         got = {}
-        z = [keep.tile([P, S], F32, name="z%d" % t) for t in range(PACK)]
-        z_bf = [keep.tile([P, HALF, PACK], BF16, name="z_bf%d" % h, align_bytes=64) for h in range(2)]
+        z = [sbuf([P, S], F32, "z%d" % t) for t in range(PACK)]
 
         def gather(t):
             for key in "cadb":
-                got[key, t] = keep.tile([P, V], F32, name="got_%s%d" % (key, t))
+                got[key, t] = sbuf([P, V], F32, "got_%s%d" % (key, t))
                 nc.vector.tensor_copy(got[key, t][:], y[t][:].indirect(lists[key][:]))
-                if key == "c":
-                    got["minus_c", t] = keep.tile([P, V], F32, name="minus_c%d" % t)
-                    nc.scalar.activation(got["minus_c", t][:], got["c", t][:], COPY, scale=-1.0)
-            got["max", t] = keep.tile([P, V], F32, name="larger%d" % t)
-            got["min", t] = keep.tile([P, V], F32, name="smaller%d" % t)
+            got["minus_c", t] = sbuf([P, V], F32, "got_minus_c%d" % t)
+            nc.scalar.activation(got["minus_c", t][:], got["c", t][:], COPY, scale=-1.0)
 
         def combine(t):
+            got["max", t] = sbuf([P, V], F32, "got_max%d" % t)
             nc.vector.tensor_tensor(got["max", t][:], got["a", t][:], got["b", t][:], ALU.max)
+            got["min", t] = sbuf([P, V], F32, "got_min%d" % t)
             nc.vector.tensor_tensor(got["min", t][:], got["b", t][:], got["d", t][:], ALU.min)
 
         def scatter(t, key):
@@ -109,52 +113,56 @@ def tile_picked_quart4_none_p_kernel(tc, x_words, x_scales, w1, w2, offs, la, lb
 
         def lay(t, h, engine_copy):
             cols = slice(h * HALF, (h + 1) * HALF)
-            if t == 2:
+            if t == 2 and h == 0:
                 engine_copy(z_bf[h][:, :, 2:4], z[t][:, cols].unsqueeze(2).to_broadcast([P, HALF, 2]))
             else:
                 engine_copy(z_bf[h][:, :, t], z[t][:, cols])
 
-        w2_bf = keep.tile([P, N, PACK], BF16, name="w2_bf", align_bytes=64)
-        w2_codes = keep.tile([P, N], U32, name="w2_codes", align_bytes=64)
-        w2_sc = keep.tile([P, N], U8, name="w2_sc", align_bytes=64)
-
         gather(0)
         gather(1)
         combine(0)
-        for u in range(PACK):
-            cols = slice(u * P, (u + 1) * P)
-            nc.scalar.copy(w2_bf[:, cols, :].rearrange("p (c i) j -> p c j i", i=4), w2_raw[:, :, cols].rearrange("p j (c i) -> p c j i", i=4))
-        combine(1)
         gather(2)
+        combine(1)
         gather(3)
         combine(2)
-        combine(3)
-        done = [0] * PACK
-        for step, t in enumerate((0, 1, 0, 1, 0, 1, 0, 2, 1, 2, 3, 2, 3, 2, 3, 3)):
-            if step == 15:
-                nc.vector.quantize_mx(w2_codes[:].bitcast(FP8X4), w2_sc[:], w2_bf[:].rearrange("p m j -> p (m j)"))
-            scatter(t, "cabd"[done[t]])
-            done[t] = done[t] + 1
-            if done[t] == 4 and t < 3:
-                lay(t, 0, nc.scalar.copy)
-                lay(t, 1, nc.scalar.copy)
+        w2_bf = sbuf([P, N, PACK], BF16, "w2_bf")
+        for u in range(PACK):
+            nc.scalar.copy(w2_bf[:, u * P : (u + 1) * P, :].rearrange("p (c i) j -> p c j i", i=4), w2_raw[u // 2][:, :, u % 2 * P : (u % 2 + 1) * P].rearrange("p j (c i) -> p c j i", i=4))
+        z_bf = [sbuf([P, HALF, PACK], BF16, "z_bf%d" % h, raw_tags[h]) for h in range(2)]
+        for pair in range(2):
+            for key in "cabd":
+                for t in (2 * pair, 2 * pair + 1):
+                    scatter(t, key)
+                    if (pair, key, t) == (0, "c", 0):
+                        combine(3)
+                    if key == "d" and t < 3:
+                        lay(t, 0, nc.scalar.copy)
+                        lay(t, 1, nc.scalar.copy)
+
+        w2_codes = sbuf([P, N], U32, "w2_codes", "got_min2")
+        w2_sc = sbuf([P, N], U8, "w2_sc")
+        nc.vector.quantize_mx(w2_codes[:].bitcast(FP8X4), w2_sc[:], w2_bf[:].rearrange("p m j -> p (m j)"))
+
+        z_codes = [sbuf([P, HALF], U32, "z_codes%d" % h) for h in range(2)]
+        z_sc = [sbuf([P, HALF], U8, "z_sc%d" % h) for h in range(2)]
+
+        def quantize_z(h):
+            nc.vector.quantize_mx(z_codes[h][:].bitcast(FP8X4), z_sc[h][:], z_bf[h][:].rearrange("p c j -> p (c j)"))
+
         lay(3, 0, nc.vector.tensor_copy)
         lay(3, 1, nc.scalar.copy)
+        quantize_z(0)
+        quantize_z(1)
 
-        z_codes = keep.tile([P, S], U32, name="z_codes", align_bytes=64)
-        z_sc = keep.tile([P, S], U8, name="z_sc", align_bytes=64)
         out_rows = out.rearrange("(u p) j -> p u j", p=P)
         for h in range(2):
             cols = slice(h * HALF, (h + 1) * HALF)
-            nc.vector.quantize_mx(z_codes[:, cols].bitcast(FP8X4), z_sc[:, cols], z_bf[h][:].rearrange("p c j -> p (c j)"))
-        for h in range(2):
-            cols = slice(h * HALF, (h + 1) * HALF)
-            for pair in range(2):
+            group = 1
+            for u0 in range(0, PACK, group):
                 acc = psum.tile([P, S], F32, name="acc", tag="bank")
-                for e in range(2):
-                    rows = slice((2 * pair + e) * P, (2 * pair + e + 1) * P)
-                    nc.tensor.matmul_mx(acc[:, e * HALF : (e + 1) * HALF], w2_codes[:, rows].bitcast(FP8X4), w2_sc[:, rows], z_codes[:, cols].bitcast(FP8X4), z_sc[:, cols], start=True, stop=True)
-                res = keep.tile([P, 2, HALF], F32, name="res%d%d" % (h, pair))
-                copy = nc.scalar.copy if pair == 0 else nc.vector.tensor_copy
-                copy(res[:].rearrange("p e c -> p (e c)"), acc[:])
-                nc.sync.dma_start(out_rows[:, 2 * pair : 2 * pair + 2, cols], res[:])
+                for e in range(group):
+                    nc.tensor.matmul_mx(acc[:, e * HALF : (e + 1) * HALF], w2_codes[:, u0 * P : (u0 + 1) * P].bitcast(FP8X4), w2_sc[:, u0 * P : (u0 + 1) * P], z_codes[h][:].bitcast(FP8X4), z_sc[h][:], start=True, stop=True)
+                res = sbuf([P, group, HALF], F32, "res%d%d" % (h, u0))
+                engine_copy = nc.vector.tensor_copy if (u0 // group) % 2 else nc.scalar.copy
+                engine_copy(res[:].rearrange("p e c -> p (e c)"), acc[:, : group * HALF])
+                nc.sync.dma_start(out_rows[:, u0 : u0 + group, cols], res[:])

from contextlib import ExitStack

import concourse.mybir as mybir

K, T, S, V, N, H = 512, 2048, 512, 128, 512, 512
FLOPS = 2 * K * H * S + 2 * H * N * S

F32 = mybir.dt.float32
BF16 = mybir.dt.bfloat16
I32 = mybir.dt.int32
U32 = mybir.dt.uint32
U16 = mybir.dt.uint16
U8 = mybir.dt.uint8
FP8X4 = mybir.dt.float8_e4m3fn_x4
ALU = mybir.AluOpType
COPY = mybir.ActivationFunctionType.Copy

P = 128
PACK = 4
HALF = S // 2


def tile_picked_quart4_none_p_kernel(tc, x_words, x_scales, w1, w2, offs, la, lb, lc, ld, out):
    nc = tc.nc
    with ExitStack() as ctx:
        keep = ctx.enter_context(tc.tile_pool(name="keep", bufs=1))
        psum = ctx.enter_context(tc.psum_pool(name="psum", bufs=8))

        def sbuf(shape, dtype, name, tag=None):
            return keep.tile(shape, dtype, name=name, tag=tag or name, align_bytes=64)

        lists = {}

        def load_list(key, src, entries):
            lists[key] = sbuf([P, entries // 16], U16, "list_" + key)
            nc.sync.dma_start(lists[key][:], src)

        load_list("offs", offs, S)

        word_table = sbuf([P, T], U32, "word_table")
        nc.sync.dma_start(word_table[:].bitcast(I32), x_words[0].rearrange("p n t -> p (n t)").bitcast(I32))
        w1_raw = sbuf([P, PACK, H], F32, "w1_raw", "w_raw")
        nc.sync.dma_start(w1_raw[:], w1.rearrange("(p j) c -> p j c", j=PACK))
        scale_table = sbuf([P, T], U8, "scale_table")
        nc.vector.memset(scale_table[:].bitcast(I32), 0)
        for q in range(4):
            nc.sync.dma_start(scale_table[32 * q : 32 * q + 4, :].bitcast(I32), x_scales[0, 4 * q : 4 * q + 4, :].bitcast(I32))
        for key, src in (("c", lc), ("a", la), ("d", ld), ("b", lb)):
            load_list(key, src, V)

        x_codes = sbuf([P, S], U32, "x_codes")
        nc.vector.tensor_copy(x_codes[:], word_table[:].indirect(lists["offs"][:]))

        w1_src = w1_raw[:].rearrange("p j (g t s i) -> p t g s j i", t=PACK, s=2, i=4)
        w1_bf, w1_codes, w1_sc = {}, {}, {}
        for t in range(PACK):
            w1_bf[t] = sbuf([P, P, PACK], BF16, "w1_bf%d" % t)
            engine_copy = nc.vector.tensor_copy if t == 0 else nc.scalar.copy
            engine_copy(w1_bf[t][:].rearrange("p (g s i) j -> p g s j i", s=2, i=4), w1_src[:, t])

        def quantize_w1(t):
            w1_codes[t] = sbuf([P, P], U32, "w1_codes%d" % t)
            w1_sc[t] = sbuf([P, P], U8, "w1_sc%d" % t)
            nc.vector.quantize_mx(w1_codes[t][:].bitcast(FP8X4), w1_sc[t][:], w1_bf[t][:].rearrange("p m j -> p (m j)"))

        x_sc = sbuf([P, S], U8, "x_sc")
        for h in range(2):
            nc.vector.tensor_copy(x_sc[:, h * HALF : (h + 1) * HALF], scale_table[:].indirect(lists["offs"][:, h * 16 : (h + 1) * 16]))
            quantize_w1(h)
        quantize_w1(2)
        quantize_w1(3)

        raw_tags = ("w_raw", "word_table")
        w2_raw = [sbuf([P, PACK, N // 2], F32, "w2_raw%d" % h, raw_tags[h]) for h in range(2)]
        w2_rows = w2.rearrange("(g t s) (h c) -> s h g t c", t=PACK, s=8, h=2)
        for s in range(8):
            for h in range(2):
                nc.sync.dma_start(w2_raw[h][s:P:8, :, :], w2_rows[s, h])

        y = [sbuf([P, S], F32, "y%d" % t) for t in range(PACK)]
        for t in range(PACK):
            for c0, width in ((0, HALF), (HALF, P), (HALF + P, P)) if t == 0 else ((0, S),):
                cols = slice(c0, c0 + width)
                acc = psum.tile([P, S], F32, name="acc", tag="bank")
                nc.tensor.matmul_mx(acc[:, :width], w1_codes[t][:].bitcast(FP8X4), w1_sc[t][:], x_codes[:, cols].bitcast(FP8X4), x_sc[:, cols], start=True, stop=True)
                engine_copy = nc.vector.tensor_copy if c0 > HALF else nc.scalar.copy
                engine_copy(y[t][:, cols], acc[:, :width])

        got = {}
        z = [sbuf([P, S], F32, "z%d" % t) for t in range(PACK)]

        def gather(t):
            for key in "cadb":
                got[key, t] = sbuf([P, V], F32, "got_%s%d" % (key, t))
                nc.vector.tensor_copy(got[key, t][:], y[t][:].indirect(lists[key][:]))
            got["minus_c", t] = sbuf([P, V], F32, "got_minus_c%d" % t)
            nc.scalar.activation(got["minus_c", t][:], got["c", t][:], COPY, scale=-1.0)

        def combine(t):
            got["max", t] = sbuf([P, V], F32, "got_max%d" % t)
            nc.vector.tensor_tensor(got["max", t][:], got["a", t][:], got["b", t][:], ALU.max)
            got["min", t] = sbuf([P, V], F32, "got_min%d" % t)
            nc.vector.tensor_tensor(got["min", t][:], got["b", t][:], got["d", t][:], ALU.min)

        def scatter(t, key):
            window = z[t][:].indirect(lists[key][:])
            if key == "a":
                nc.vector.tensor_tensor(window, got["a", t][:], got["minus_c", t][:], ALU.add)
            elif key == "c":
                nc.vector.tensor_tensor(window, got["c", t][:], got["d", t][:], ALU.add)
            else:
                nc.vector.tensor_copy(window, got["max" if key == "b" else "min", t][:])

        def lay(t, h, engine_copy):
            cols = slice(h * HALF, (h + 1) * HALF)
            if t == 2 and h == 0:
                engine_copy(z_bf[h][:, :, 2:4], z[t][:, cols].unsqueeze(2).to_broadcast([P, HALF, 2]))
            else:
                engine_copy(z_bf[h][:, :, t], z[t][:, cols])

        gather(0)
        gather(1)
        combine(0)
        gather(2)
        combine(1)
        gather(3)
        combine(2)
        w2_bf = sbuf([P, N, PACK], BF16, "w2_bf")
        for u in range(PACK):
            nc.scalar.copy(w2_bf[:, u * P : (u + 1) * P, :].rearrange("p (c i) j -> p c j i", i=4), w2_raw[u // 2][:, :, u % 2 * P : (u % 2 + 1) * P].rearrange("p j (c i) -> p c j i", i=4))
        z_bf = [sbuf([P, HALF, PACK], BF16, "z_bf%d" % h, raw_tags[h]) for h in range(2)]
        for pair in range(2):
            for key in "cabd":
                for t in (2 * pair, 2 * pair + 1):
                    scatter(t, key)
                    if (pair, key, t) == (0, "c", 0):
                        combine(3)
                    if key == "d" and t < 3:
                        lay(t, 0, nc.scalar.copy)
                        lay(t, 1, nc.scalar.copy)

        w2_codes = sbuf([P, N], U32, "w2_codes", "got_min2")
        w2_sc = sbuf([P, N], U8, "w2_sc")
        nc.vector.quantize_mx(w2_codes[:].bitcast(FP8X4), w2_sc[:], w2_bf[:].rearrange("p m j -> p (m j)"))

        z_codes = [sbuf([P, HALF], U32, "z_codes%d" % h) for h in range(2)]
        z_sc = [sbuf([P, HALF], U8, "z_sc%d" % h) for h in range(2)]

        def quantize_z(h):
            nc.vector.quantize_mx(z_codes[h][:].bitcast(FP8X4), z_sc[h][:], z_bf[h][:].rearrange("p c j -> p (c j)"))

        lay(3, 0, nc.vector.tensor_copy)
        lay(3, 1, nc.scalar.copy)
        quantize_z(0)
        quantize_z(1)

        out_rows = out.rearrange("(u p) j -> p u j", p=P)
        for h in range(2):
            cols = slice(h * HALF, (h + 1) * HALF)
            group = 1
            for u0 in range(0, PACK, group):
                acc = psum.tile([P, S], F32, name="acc", tag="bank")
                for e in range(group):
                    nc.tensor.matmul_mx(acc[:, e * HALF : (e + 1) * HALF], w2_codes[:, u0 * P : (u0 + 1) * P].bitcast(FP8X4), w2_sc[:, u0 * P : (u0 + 1) * P], z_codes[h][:].bitcast(FP8X4), z_sc[h][:], start=True, stop=True)
                res = sbuf([P, group, HALF], F32, "res%d%d" % (h, u0))
                engine_copy = nc.vector.tensor_copy if (u0 // group) % 2 else nc.scalar.copy
                engine_copy(res[:].rearrange("p e c -> p (e c)"), acc[:, : group * HALF])
                nc.sync.dma_start(out_rows[:, u0 : u0 + group, cols], res[:])
